import numpy as np
CORES = [3,7,11,15,131,135,139,143]
N = 8
T, FF, CAP, CAPP = 4096, 4, 1024, 256
def entries(a): return a.T.reshape(-1)
def pack(v, P): return np.ascontiguousarray(np.asarray(v, np.int32).reshape(-1, P).T)
def lists(rng, how):
    O = np.stack([rng.permutation(np.repeat(np.arange(N), CAPP))[:CAP] for k in range(N)])
    if how == "apart": s = int(rng.integers(N * CAPP - CAP + 1)); cnt = np.bincount(np.repeat(np.arange(N), CAPP)[s:s + CAP], minlength=N); a = rng.permutation(N); O = np.stack([rng.permutation(np.repeat(np.arange(N), cnt[(a + k) % N])) for k in rng.permutation(N)])
    if how == "full": z = rng.permutation(N); O = np.stack([rng.permutation(np.repeat(z, CAPP)[:CAP]) for k in range(N)])
    if how == "none": z = int(rng.integers(N)); O = np.stack([rng.permutation(np.repeat(np.delete(np.arange(N), z), CAPP))[:CAP] for k in range(N)])
    P = np.zeros((N, CAP), np.int64)
    for o in range(N):
        q = rng.permutation(T); u = 0
        for k in range(N):
            m = np.nonzero(O[k] == o)[0]
            if how != "apart": q = rng.permutation(T); u = 0
            if how == "sorted": q = np.r_[0, T - 1, 1 + rng.permutation(T - 2)]
            P[k, m] = T * o + q[u:u + len(m)]; u += len(m)
    if how == "same": P = np.stack([rng.permutation(P[0]) for k in range(N)])
    if how == "sorted": P = np.sort(P, axis=1)
    G = 2 * rng.random((N, 16, CAP // 16), dtype=np.float32) - 1
    if how == "none": G[rng.random(G.shape) < 0.125] = 0
    return {"gate": G, "pick": np.stack([pack(p, 16) for p in P])}
def setup_inputs(rng):
    return dict({"x": rng.standard_normal((N, 128, T), dtype=np.float32), "w1": (rng.standard_normal((N, 128, FF * 128), dtype=np.float32) / 8), "w2": (rng.standard_normal((N, 128, FF * 128), dtype=np.float32) / 16)}, **lists(rng, "uniform"))
def setup_inputs_apart(rng):
    d = setup_inputs(rng); d.update(lists(rng, "apart"))
    for k in ("x",): d[k] = (d[k].astype(np.float32) * 1024.0).astype(d[k].dtype)
    return d
def setup_inputs_full(rng):
    d = setup_inputs(rng); d.update(lists(rng, "full"))
    for k in ("x",): d[k] = (d[k].astype(np.float32) * (1 / 1024.0)).astype(d[k].dtype)
    return d
def setup_inputs_none(rng):
    d = setup_inputs(rng); d.update(lists(rng, "none"))
    return d
def setup_inputs_same(rng):
    d = setup_inputs(rng); d.update(lists(rng, "same"))
    return d
def setup_inputs_sorted(rng):
    d = setup_inputs(rng); d.update(lists(rng, "sorted"))
    return d
def check_inputs(x):
    bad = []
    if x["pick"].min() < 0 or x["pick"].max() >= N * T: bad.append("pick out of range")
    if any(len(np.unique(a)) != a.size for a in x["pick"]): bad.append("a token stands twice in a list")
    if max(int(np.bincount(entries(a) // T, minlength=N).max()) for a in x["pick"]) > CAPP: bad.append("more than CAPP of an expert's tokens lie on one rank")
    return bad
def reference(x, w1, w2, gate, pick):
    X, W1, W2 = x.astype(np.float64), w1.astype(np.float64), w2.astype(np.float64)
    A = np.concatenate(list(X), axis=1); Y = np.zeros((128, N * T))
    for k in range(N):
        P = entries(pick[k]); g = entries(gate[k]).astype(np.float64)
        Y[:, P] += g[None, :] * sum(W2[k][:, 128 * f:128 * f + 128].T @ np.maximum(W1[k][:, 128 * f:128 * f + 128].T @ A[:, P], 0.0) for f in range(FF))
    return {"y": np.stack([Y[:, T * r:T * r + T] for r in range(N)]).astype(np.float32)}

@@ -1,0 +1,566 @@
+from concourse.bass import DstId, RemoteDMATransfer
+from concourse.mybir import AluOpType as Op, ActivationFunctionType as AF
+
+WORLD = 256
+SCRATCH, AT = {}, {}
+for _d, _s in (("float32", "WB:1024 WS:1024 XB:4352 YB:4096 R:2064 VB:512 VS:1792 RES:512 GTE:8 LST:128 GMT:16"),
+               ("int32", "PKI:8"), ("uint16", "OFF:128 PREV:128 INV:256 XOFF:128"), ("bfloat16", "MAP:4352 GT:2048")):
+    for _x in _s.split():
+        _n, _w = _x.split(":")
+        SCRATCH[_n] = ("sbuf", [128, int(_w)], _d)
+        AT[_n] = (_n, 0, int(_w))
+for _b, _d, _s in (
+        ("TF", "float32", "GB:512 HS:1024 PF:1 P16F:1 PMF:1 PMF16:1 PGF:1 P8F:1 IOM:128 IO16:16 IOC:16 L0:16 TOKM:8 SO:64 SA:32 "
+         "SB:16 D16:8 COLF:8 VAL:8 LT:1024 RH:128 RG:128 RM16:128 SELT:128 MSI:256 MSK:256 SGA:128 SGB:128 REPG:256 "
+         "GX:256 XF:128 DMI:128 DM:128 XM:128 XA:64 XC:32 XD:16 PCI:8 K128:256 BASE:128 ZA:128 ZB:128 ZC:128 ZD:128 "
+         "ZE:128 ZT1:64 ZT2:32 ZT3:16 PT:16 YA:256 YBB:256 YC:256 YT1:128 YT2:64 YT3:32 IT:32 C8F:16 M8I:256 M8:256 "
+         "P16I:128 P16:128 PTR:128 PTM:128 ITR:256 ITM:256"),
+        ("TI", "int32", "PM4:4 PM4b:4 PMI:1 PGI:1 P8I:1 OCOL:64 N8:64 OW16:8 OW256:8 TOKI:8 OWR:64 SEL:8 H16:8 C16I:16 "
+         "PGW:128 PGW4:128 C8I:16"),
+        ("TU", "uint16", "RO8:4 C16:16 E16:16 C8:16"),
+        ("TB", "bfloat16", "SM:64 TRI:128 ONES:128 OB:66 EX:64 VALS:256 PICK:8")):
+    _o = 0
+    for _x in _s.split():
+        _n, _w = _x.split(":")
+        AT[_n] = (_b, _o, int(_w))
+        _o += (int(_w) + 7) // 8 * 8
+    SCRATCH[_b] = ("sbuf", [128, _o], _d)
+for _i in range(8):
+    SCRATCH["p%d" % _i] = ("psum", [128, 512], "float32")
+    AT["p%d" % _i] = ("p%d" % _i, 0, 512)
+SEMAPHORES = (["aW%d" % f for f in range(4)] + ["aS%d" % f for f in range(4)] + ["aR%d" % n for n in range(16)]
+              + ["aL", "aG", "aV0", "aV1", "aX", "aP", "aI", "ls"] + ["q%d" % i for i in range(32)])
+
+
+def bits(mask):
+    return [1 << b for b in range(32) if mask >> b & 1]
+
+
+def dep_scan(rec, q, rd, wr):
+    deps = []
+    ops = rec["ops"]
+    inorder = q in ("V", "P", "S", "G")
+    for regs, w in ((rd, False), (wr, True)):
+        for name, lo, hi in regs:
+            ps = name[0] == "p"
+            for alo, ahi, aid, aw in rec["acc"].get(name, []):
+                same = inorder and ops[aid]["q"] == q and ops[aid]["kind"] == "c"
+                over = alo < hi and lo < ahi
+                if same:
+                    need = over and aw and not w
+                elif ps:
+                    need = True
+                else:
+                    need = over and (aw or w)
+                if need and aid not in deps:
+                    deps.append(aid)
+    return deps
+
+
+def op(rec, q, fn, rd=(), wr=(), kind="c", deps=(), sem=None, cnt=0):
+    d = dep_scan(rec, q, rd, wr) if kind != "r" else []
+    d += [x for x in deps if x not in d]
+    me = len(rec["ops"])
+    rec["ops"].append({"q": q, "fn": fn, "deps": d, "kind": kind, "sem": sem, "cnt": cnt})
+    for regs, w in ((rd, False), (wr, True)):
+        for name, lo, hi in regs:
+            rec["acc"].setdefault(name, []).append((lo, hi, me, w))
+    return me
+
+
+def emit(rec, g, T):
+    eng = {"V": g.vector, "P": g.tensor, "S": g.scalar, "Y": g.sync, "G": g}
+    known = {q: set() for q in eng}
+    after, plan, waited = {}, [], set()
+    for i, o in enumerate(rec["ops"]):
+        if o["kind"] == "r":
+            after[i] = {i}
+            continue
+        k = known[o["q"]]
+        ws = []
+        for d in sorted(o["deps"], reverse=True):
+            if d not in k:
+                ws.append(d)
+                k |= after[d]
+                waited.add(d)
+        after[i] = k | {i}
+        plan.append((i, o, ws))
+    taken = {o["sem"] for o in rec["ops"]} | {"ls"}
+    pool = [s for s in reversed(SEMAPHORES) if s not in taken]
+    sem, tails = {}, []
+    for i, o in enumerate(rec["ops"]):
+        assert o["kind"] != "r" or i in waited, "an arrival that nobody waits for"
+        if i not in waited:
+            continue
+        if o["kind"] == "r":
+            sem[i] = (T.sem[o["sem"]], o["cnt"])
+            continue
+        assert o["kind"] in ("c", "d"), "a send is never waited for"
+        for x in tails:
+            if x[0] in after[i] and x[3] == o["kind"]:
+                break
+        else:
+            x = [None, 0, T.sem[pool[len(tails)]], o["kind"]]
+            tails.append(x)
+        x[0], x[1] = i, x[1] + (16 if o["kind"] == "d" else 1)
+        sem[i] = (x[2], x[1])
+    for i, o, ws in plan:
+        e = eng[o["q"]]
+        for d in ws:
+            e.wait_ge(sem[d][0], sem[d][1])
+        if o["fn"] is not None:
+            ins = o["fn"](e)
+            if i in sem:
+                ins.then_inc(sem[i][0], 16 if o["kind"] == "d" else 1)
+    if rec["ls"]:
+        g.wait_ge(T.sem["ls"], rec["ls"])
+
+
+def make_plan(T, topo):
+    cores = T.cores
+    R = range(len(cores))
+    key = lambda c: (topo.host(c), topo.chip(c))
+    chips = list(dict.fromkeys(key(c) for c in cores))
+    place, spread, index, pair, third, used = {}, {}, {}, {}, {}, set()
+    for r, rc in enumerate(cores):
+        k = key(rc)
+        pair[k] = [s for s in R if key(cores[s]) == k]
+        peers = [c for c in range(WORLD) if key(c) == k and topo.die(c) == topo.die(rc) and c != rc]
+        like = [e for e in R if e != r and topo.die(cores[e]) == topo.die(rc)]
+        mate = [e for e in like if topo.mates(cores[e], rc)][0]
+        plane = [e for e in like if topo.same_plane(cores[e], rc)][0]
+        diag = [e for e in like if e not in (mate, plane)][0]
+        port = [c for c in peers if topo.may_write(c, cores[mate])][0]
+        rest = [c for c in peers if c != port]
+        a = pair[k].index(r)
+        for e, c, h in ((r, rc, 1 - a), (plane, port, a), (mate, rest[0], 1 - a), (diag, rest[1], a)):
+            place[(k, e)] = c
+            third[(k, e)] = h
+        spread[r] = port
+        x = [c for c in range(WORLD) if topo.same_plane(c, rc) and topo.host(c) == topo.host(rc)
+             and topo.die(c) == topo.die(rc) and key(c) not in chips and c not in used][0]
+        used.add(x)
+        index[r] = x
+    pos = {}
+    for r, rc in enumerate(cores):
+        k = key(rc)
+        a = pair[k].index(r)
+        order = [e for e in R if third[(k, e)] == a] + [e for e in R if third[(k, e)] != a and e != r] + [r]
+        pos[r] = {e: i for i, e in enumerate(order)}
+    return key, chips, place, spread, index, pair, third, pos
+
+
+def rank_program(g, core, T, topo):
+    keyof, chips, place, spread, index, pair, third, allpos = make_plan(T, topo)
+    key = keyof(core)
+    me = T.rank_of(core)
+    rec = {"ops": [], "acc": {}, "ls": 0}
+    cores = T.cores
+    N = len(cores)
+
+    def t(name, lo=None, hi=None, step=1):
+        b, o, n = AT[name]
+        lo, hi = (0, n) if lo is None else (lo, hi)
+        return T[b][:, o + lo:o + hi] if step == 1 else T[b][:, o + lo:o + hi:step]
+
+    def al(name):
+        return (name, 0, AT[name][2])
+
+    def V(fn, rd, wr):
+        return op(rec, "V", fn, rd, wr)
+
+    def dst(c):
+        rid, pid = topo.addr(c, core)
+        return DstId(rid=rid, pnc=pid)
+
+    def send(trs, rd):
+        rec["ls"] += sum(len(x[0]) for x in trs)
+
+        def fn(e):
+            ts = [RemoteDMATransfer(dst_ids=[dst(c) for c, _ in ds], dma_engine_mask=sum(bs), remote_sem=T.sem[s],
+                                    srcs=[src], dsts=[d for _, d in ds], alu_op=0) for bs, s, src, ds in trs]
+            return e.remote_dma_fused(ts, local_sem=T.sem["ls"])
+        op(rec, "G", fn, rd, (), "s")
+
+    def arrive(sem, cnt, regs):
+        op(rec, "R", None, (), regs, "r", (), sem, cnt)
+
+    def iota(name, pattern, base=0, cm=0):
+        op(rec, "G", lambda e: e.iota(t(name), pattern, base, cm, allow_small_or_imprecise_dtypes=True), (), [al(name)])
+
+    def full(x):
+        return al(x) if isinstance(x, str) else x
+
+    def ts(out, in0, s1, s2, op0, op1=None):
+        out, in0 = full(out), full(in0)
+        sc = [full(s) for s in (s1, s2)]
+        rd = [in0] + [s for s in sc if isinstance(s, tuple)]
+        sc = [t(*s) if isinstance(s, tuple) else s for s in sc]
+        if op1 is None:
+            V(lambda e: e.tensor_scalar(t(*out), t(*in0), sc[0], None, op0), rd, [out])
+        else:
+            V(lambda e: e.tensor_scalar(t(*out), t(*in0), sc[0], sc[1], op0, op1), rd, [out])
+
+    def tt(out, a, b, o):
+        out, a, b = full(out), full(a), full(b)
+        V(lambda e: e.tensor_tensor(t(*out), t(*a), t(*b), o), [a, b], [out])
+
+    def cp(out, a):
+        out, a = full(out), full(a)
+        V(lambda e: e.tensor_copy(t(*out), t(*a)), [a], [out])
+
+    def fill(r, v):
+        r = full(r)
+        V(lambda e: e.memset(t(*r), v), [], [r])
+
+    def mm(out, lhs, rhs, start, stop):
+        lhs, rhs = full(lhs), full(rhs)
+        op(rec, "P", lambda e: e.matmul(t(*out), t(*lhs), t(*rhs), start, stop), [lhs, rhs], [out])
+
+    def gather(q, out, win, off):
+        out, win, off = full(out), full(win), full(off)
+        if q == "V":
+            fn = lambda e: e.tensor_copy(t(*out), t(*win).indirect(t(*off)))
+        else:
+            fn = lambda e: e.activation(t(*out), t(*win).indirect(t(*off)), AF.Copy)
+        op(rec, q, fn, [win, off], [out])
+
+    def part_consts():
+        iota("PM4", [[0, 4]], 0, 1)
+        cp("PF", ("PM4", 0, 1))
+        ts("PMI", ("PM4", 0, 1), 15, None, Op.bitwise_and)
+        cp("PMF", "PMI")
+        ts("PGI", ("PM4", 0, 1), 4, None, Op.logical_shift_right)
+        cp("PGF", "PGI")
+
+    for r in range(N):
+        if index[r] != core:
+            continue
+        ob = bits(topo.mask(core, cores[r]))
+        arrive("aX", len(ob), [al("XOFF")])
+        part_consts()
+        iota("DMI", [[1, 8], [0, 16]])
+        iota("VALS", [[1, 256]])
+        iota("PCI", [[16, 8]])
+        iota("K128", [[0, 32], [128, 8]], 1)
+        iota("BASE", [[128, 8], [1024, 2], [0, 8]])
+        iota("C8I", [[2, 16]])
+        iota("M8I", [[0, 32], [1, 8]])
+        iota("P16I", [[0, 8], [1, 16]])
+        fill("MAP", -32768.0)
+        ts("DM", "DMI", "PGF", None, Op.is_equal)
+        ts("PICK", "PCI", "PF", None, Op.is_equal)
+        ts("P8I", ("PM4", 0, 1), 3, 1, Op.logical_shift_right, Op.bitwise_and)
+        cp("P8F", "P8I")
+        ts("C8F", "C8I", "P8F", None, Op.add)
+        cp("C8", "C8F")
+        ts("M8", "M8I", "PGF", None, Op.is_equal)
+        ts("P16", "P16I", "PMF", None, Op.is_equal)
+        cp("XF", "XOFF")
+        tt("XM", "XF", "DM", Op.mult)
+        tt("XA", ("XM", 0, 64), ("XM", 64, 128), Op.add)
+        tt("XC", ("XA", 0, 32), ("XA", 32, 64), Op.add)
+        tt("XD", ("XC", 0, 16), ("XC", 16, 32), Op.add)
+        cp("E16", "XD")
+        V(lambda e: e.tensor_copy(t("MAP").indirect(t("E16")), t("VALS")), [al("VALS"), al("E16"), al("MAP")], [al("MAP")])
+        for b in range(32):
+            mm(("p0", 8 * b, 8 * b + 8), ("MAP", 128 * b, 128 * b + 128), "PICK", True, True)
+        for h in range(4):
+            gather("SV"[h % 2], ("GT", 512 * h, 512 * h + 512), "MAP", ("XOFF", 32 * h, 32 * h + 32))
+        for b in range(16):
+            mm(("p1", 8 * b, 8 * b + 8), ("GT", 128 * b, 128 * b + 128), "PICK", True, True)
+
+        def tree(src, a, n):
+            for d in a:
+                n //= 2
+                V(lambda e, s=src, d=d, n=n: e.tensor_tensor(t(d), t(s, 0, 2 * n, 2), t(s, 1, 2 * n, 2), Op.max),
+                  [al(src)], [al(d)])
+                src = d
+
+        def wrap(cols, src, rep, prod, bank, n, out, sem):
+            ts(cols, src, 0.0, 3.0, Op.max, Op.add)
+            gather("V", rep, cols, ("C8", 0, n // 16))
+            tt(prod, rep, ("M8", 0, n), Op.mult)
+            mm((bank, 0, n), "P16", prod, True, True)
+            cp(out, (bank, 0, n))
+            send([(ob, sem, t(out), [(cores[r], t(out))])], [al(out)])
+        ts("ZA", ("p1", 0, 128), 127.5, 896.0, Op.is_gt, Op.mult)
+        tt("ZB", ("p1", 0, 128), "ZA", Op.add)
+        tt("ZC", "ZB", ("K128", 0, 128), Op.add)
+        tt("ZD", "ZC", "BASE", Op.is_le)
+        tt("ZE", "ZD", "ZC", Op.mult)
+        tree("ZE", ("ZT1", "ZT2", "ZT3"), 128)
+        wrap("PT", "ZT3", "PTR", "PTM", "p2", 128, "PREV", "aP")
+        ts("YA", ("p0", 0, 256), 127.5, 896.0, Op.is_gt, Op.mult)
+        tt("YBB", ("p0", 0, 256), "YA", Op.add)
+        tt("YC", "YBB", "K128", Op.add)
+        tree("YC", ("YT1", "YT2", "YT3"), 256)
+        wrap("IT", "YT3", "ITR", "ITM", "p3", 256, "INV", "aI")
+        emit(rec, g, T)
+        return
+    if key not in chips:
+        return
+
+    two = pair[key]
+    E = [e for (k, e), c in place.items() if c == core][0]
+    home = cores[E]
+    elsewhere = [place[(k, E)] for k in chips if place[(k, E)] != home]
+    OFFB = bits(topo.mask(core, [c for c in cores if keyof(c) != key and topo.may_write(core, c)][0]))
+    ONB = bits(topo.mask(core, [place[(key, e)] for e in range(N) if e != E][0]))
+    HIB = [b for b in ONB if b not in OFFB]
+    half = len(OFFB) // 2
+    spread_for = [r for r in two if spread[r] == core]
+
+    if me is None:
+        near = topo.mates(core, home) or topo.same_plane(core, home)
+        for f in range(4):
+            arrive("aW%d" % f, half if near else len(OFFB), [("WB", 256 * f, 256 * f + 256)])
+            if spread_for:
+                arrive("aS%d" % f, len(HIB), [("WS", 256 * f, 256 * f + 256)])
+        arrive("aG", len(OFFB), [al("GMT")])
+    for p in range(2):
+        froms = [a for a in range(2) if two[a] != me]
+        arrive("aV%d" % p, 2 * len(froms), [("VB", 256 * p + 128 * a, 256 * p + 128 * a + 128) for a in froms])
+    if me is not None:
+        pos = allpos[me]
+        arrive("aL", len(OFFB) * (N - 2) + len(HIB), [("LST", 16 * pos[e], 16 * pos[e] + 16) for e in range(N) if e != me])
+        arrive("aP", len(OFFB), [al("PREV")])
+        arrive("aI", len(OFFB), [al("INV")])
+        for n in range(16):
+            for e in range(N):
+                if e != me and pos[e] == n % 8:
+                    arrive("aR%d" % n, len(ONB) if n >= 8 or e in two else len(ONB) // 2, [("R", 4 + 128 * n, 132 + 128 * n)])
+
+    def gate_iotas():
+        iota("C16I", [[1, 16]])
+        iota("MSI", [[0, 16], [1, 16]])
+        iota("PGW", [[0, 128]], 0, 1)
+
+    def gate_consts():
+        cp("C16", "C16I")
+        ts("MSK", "MSI", "PMF", None, Op.is_equal)
+        ts("PGW4", "PGW", 4, None, Op.logical_shift_right)
+        ts("SGA", "PGW4", float(two[0]), None, Op.is_equal)
+        ts("SGB", "PGW4", float(two[1]), None, Op.is_equal)
+
+    def gates_prepare():
+        gather("V", "REPG", "GMT", "C16")
+        tt("GX", "REPG", "MSK", Op.mult)
+
+    order = [third[(key, E)], 1 - third[(key, E)]]
+    blocks = [(0, 256)] + [(256 + 128 * a, 384 + 128 * a) for a in order]
+
+    def expert():
+        units = [(b, f) for b in range(3) for f in range(4)]
+        LAG = 2
+
+        def l2(u):
+            b, f = units[u]
+            n = blocks[b][1] - blocks[b][0]
+            s = 256 * (u % 4)
+            mm(("p%d" % (4 + b), 0, n), ("WB", 256 * f + 128, 256 * f + 256), ("HS", s, s + n), f == 0, f == 3)
+        for u, (b, f) in enumerate(units):
+            lo, hi = blocks[b]
+            n = hi - lo
+            h = "p%d" % (u % 4)
+            s = 256 * (u % 4)
+            mm((h, 0, n), ("WB", 256 * f, 256 * f + 128), ("VB", lo, hi), True, True)
+            op(rec, "S", lambda e, h=h, n=n, s=s: e.activation(t("HS", s, s + n), t(h, 0, n), AF.Relu),
+               [(h, 0, n)], [("HS", s, s + n)])
+            if u >= LAG:
+                l2(u - LAG)
+            if u == 4:
+                for p in range(2):
+                    for a in range(2):
+                        mm(("p7", 256 * p + 128 * a, 256 * p + 128 * a + 128), "SG" + "AB"[a],
+                           ("GX", 128 * p, 128 * p + 128), True, True)
+                cp("GB", "p7")
+        for u in range(len(units) - LAG, len(units)):
+            l2(u)
+
+    def rcol(a, p):
+        n = 8 * p + allpos[two[a]][E]
+        return n, 4 + 128 * n
+
+    def across(c):
+        return topo.die(c) != topo.die(core)
+
+    if me is None:
+        part_consts()
+        gate_iotas()
+        gate_consts()
+        gates_prepare()
+
+        def forward(f):
+            w, d = t("WS", 256 * f, 256 * f + 256), t("WB", 256 * f, 256 * f + 256)
+            to = [place[(k, spread_for[0])] for k in chips if k != key]
+            m = [c for c in to if topo.mates(core, c)][0]
+            s = [c for c in to if topo.same_plane(core, c)][0]
+            send([(OFFB[:half], "aW%d" % f, w, [(m, d)]), (OFFB[half:], "aW%d" % f, w, [(s, d)])],
+                 [("WS", 256 * f, 256 * f + 256)])
+
+        def relay(f):
+            w = t("WB", 256 * f, 256 * f + 256)
+            c = [x for x in elsewhere if not topo.mates(home, x) and not topo.same_plane(home, x)][0]
+            send([(OFFB, "aW%d" % f, w, [(c, w)])], [("WB", 256 * f, 256 * f + 256)])
+        if spread_for:
+            forward(0)
+            forward(1)
+            forward(2)
+            relay(1)
+            forward(3)
+            relay(3)
+        elif topo.mates(core, home):
+            relay(0)
+            relay(2)
+        expert()
+        for b, (lo, hi) in enumerate(blocks):
+            tt(("RES", lo, hi), ("p%d" % (4 + b), 0, hi - lo), ("GB", lo, hi), Op.mult)
+            trs = []
+            for a in (0, 1) if b == 0 else (order[b - 1],):
+                n, c0 = rcol(a, 0 if b == 0 else 1)
+                eng = ONB if b else ONB[0::2] if across(cores[two[a]]) else ONB[1::2]
+                s = 128 * a if b == 0 else lo
+                trs.append((eng, "aR%d" % n, t("RES", s, s + 128), [(cores[two[a]], t("R", c0, c0 + 128))]))
+            send(trs, [("RES", lo, hi)])
+        emit(rec, g, T)
+        return
+
+    mya = two.index(me)
+    oth = 1 - mya
+
+    def load(out, src):
+        return op(rec, "Y", lambda e: e.dma_start(t(*out), src), (), [out], "d")
+    load(al("PKI"), T.pick[:])
+    load(al("GTE"), T.gate[:])
+    for f in range(4):
+        load(("WB", 256 * f, 256 * f + 128), T.w1[:, 128 * f:128 * f + 128])
+        load(("WB", 256 * f + 128, 256 * f + 256), T.w2[:, 128 * f:128 * f + 128])
+        load(("XB", 1024 * f, 1024 * f + 1024), T.x[:, 1024 * f:1024 * f + 1024])
+
+    iota("PM4", [[0, 4]], 0, 1)
+    iota("OCOL", [[16, 8], [0, 8]])
+    iota("N8", [[0, 8], [1, 8]])
+    iota("IOM", [[16, 128]])
+    iota("IO16", [[1, 16]])
+    iota("IOC", [[1, 16]], 4096)
+    iota("RM16", [[0, 8], [1, 16]], 16 * me)
+    gate_iotas()
+    fill(("OB", 0, 2), 0.0)
+    fill("ONES", 1.0)
+    ts("PM4b", "PM4", 7, None, Op.bitwise_and)
+    cp("RO8", "PM4b")
+    cp("PF", ("PM4", 0, 1))
+    ts("P16F", ("PM4", 0, 1), 16.0, None, Op.mult)
+    ts("PMI", ("PM4", 0, 1), 15, None, Op.bitwise_and)
+    ts("SM", "N8", 0.0, None, Op.is_gt)
+    ts("TRI", "IOM", "P16F", None, Op.is_gt)
+    cp("PMF", "PMI")
+    ts("PMF16", "PMI", 16.0, None, Op.mult)
+    ts("L0", "IOC", "PMF16", None, Op.add)
+
+    ts("OW16", "PKI", 8, 0xF0, Op.logical_shift_right, Op.bitwise_and)
+    gather("V", "OWR", "OW16", "RO8")
+    tt(("OB", 2, 66), "OWR", "OCOL", Op.is_equal)
+    mm(("p0", 0, 64), "TRI", ("OB", 2, 66), True, False)
+    V(lambda e: e.tensor_tensor_scan(t("EX"), t("OB", 1, 65), t("SM"), 0.0, Op.add, Op.mult), [al("OB"), al("SM")], [al("EX")])
+    mm(("p0", 0, 64), "ONES", "EX", False, True)
+    ts("OW256", "PKI", 4, 0xF00, Op.logical_shift_right, Op.bitwise_and)
+    ts("TOKI", "PKI", 4095, None, Op.bitwise_and)
+    ts("TOKM", "TOKI", 4096.0, None, Op.subtract)
+    tt("SO", ("p0", 0, 64), ("OB", 2, 66), Op.mult)
+    tt("SA", ("SO", 0, 32), ("SO", 32, 64), Op.add)
+    tt("SB", ("SA", 0, 16), ("SA", 16, 32), Op.add)
+    tt("SEL", ("SB", 0, 8), ("SB", 8, 16), Op.add)
+    ts("H16", "SEL", 0xF0, None, Op.bitwise_and)
+    tt("VAL", "TOKM", "SEL", Op.subtract)
+    tt("D16", "H16", "OW256", Op.add)
+    tt("COLF", "SEL", "H16", Op.subtract)
+    for q in range(8):
+        ts(("RH", 16 * q, 16 * q + 16), "IO16", ("COLF", q, q + 1), ("VAL", q, q + 1), Op.is_equal, Op.mult)
+        ts(("LT", 128 * q, 128 * q + 128), "IOM", ("D16", q, q + 1), None, Op.is_equal)
+        mm(("p1", 0, 16), ("LT", 128 * q, 128 * q + 128), ("RH", 16 * q, 16 * q + 16), q == 0, q == 7)
+    mine = ("LST", 16 * pos[me], 16 * pos[me] + 16)
+    tt(mine, ("p1", 0, 16), "L0", Op.add)
+
+    def weights(f):
+        w = ("WB", 256 * f, 256 * f + 256)
+        send([(HIB, "aS%d" % f, t(*w), [(spread[me], t("WS", w[1], w[2]))])], [w])
+    weights(0)
+    weights(1)
+    to = [(e, t("LST", 16 * allpos[e][me], 16 * allpos[e][me] + 16)) for e in list(range(me + 1, N)) + list(range(me))]
+    send([(OFFB, "aL", t(*mine), [(cores[e], d) for e, d in to if e not in two]),
+          (HIB, "aL", t(*mine), [(cores[e], d) for e, d in to if e in two])], [mine])
+    weights(2)
+    weights(3)
+
+    ts("SELT", "RM16", "PF", None, Op.is_equal)
+    for q in range(8):
+        ts(("RG", 16 * q, 16 * q + 16), "IO16", ("COLF", q, q + 1), ("GTE", q, q + 1), Op.is_equal, Op.mult)
+        mm(("p2", 0, 16), ("LT", 128 * q, 128 * q + 128), ("RG", 16 * q, 16 * q + 16), q == 0, q == 7)
+    cp("GMT", ("p2", 0, 16))
+    fill(("XB", 4096, 4352), 0.0)
+    fill(("R", 0, 4), 0.0)
+    gate_consts()
+    gates_prepare()
+
+    mm(("p3", 0, 128), "SELT", "LST", True, True)
+    cp("OFF", ("p3", 0, 128))
+    others = [e for e in range(N) if e != me]
+    crossing = [e for e in others if across(place[(key, e)])]
+    staying = [e for e in others if e not in crossing]
+    engines = {e: ONB[0::2][2 * i:2 * i + 2] for i, e in enumerate(crossing)}
+    engines.update({e: ONB[1::2][2 * i:2 * i + 2] for i, e in enumerate(staying)})
+    for p in range(2):
+        v = 256 * p + 128 * mya
+        trs = []
+        for i, e in enumerate(others + [me]):
+            c = 16 * pos[e] + 8 * p
+            s = ("VB", v, v + 128) if e == me else ("VS", 896 * p + 128 * i, 896 * p + 128 * i + 128)
+            gather("VS"[i % 2], s, "XB", ("OFF", c, c + 8))
+            if e != me:
+                trs.append((engines[e], "aV%d" % p, t(*s), [(place[(key, e)], t("VB", v, v + 128))]))
+        send(trs, [("VS", 896 * p, 896 * p + 896)])
+        if p == 0:
+            send([(OFFB, "aX", t("OFF"), [(index[me], t("XOFF"))])], [al("OFF")])
+            send([(OFFB, "aG", t("GMT"), [(c, t("GMT")) for c in elsewhere])], [al("GMT")])
+
+    expert()
+
+    def scale(b, a):
+        p = 0 if b == 0 else 1
+        o = ("p%d" % (4 + b), 128 * a, 128 * a + 128) if b == 0 else ("p%d" % (4 + b), 0, 128)
+        gb = ("GB", 256 * p + 128 * a, 256 * p + 128 * a + 128)
+        n, c0 = rcol(a, p)
+        if a == mya:
+            tt(("R", c0, c0 + 128), o, gb, Op.mult)
+        else:
+            s = ("RES", gb[1], gb[2])
+            tt(s, o, gb, Op.mult)
+            send([(ONB, "aR%d" % n, t(*s), [(cores[two[a]], t("R", c0, c0 + 128))])], [s])
+
+    def chain(n):
+        if n == 0:
+            return
+        k, p = n % 8, n // 8
+        u = 4 + 128 * n
+        V(lambda e: e.tensor_tensor(t("R", u, u + 128), t("R", 0, u).indirect(t("PREV", 16 * k + 8 * p, 16 * k + 8 * p + 8)),
+                                    t("R", u, u + 128), Op.add),
+          [("R", 0, u + 128), al("PREV")], [("R", u, u + 128)])
+    scale(0, oth)
+    scale(0, mya)
+    scale(1, oth)
+    for n in range(12):
+        chain(n)
+    scale(2, mya)
+    for n in range(12, 16):
+        chain(n)
+    lo = 0
+    stores = []
+    for i, w in enumerate([256, 256] + [512] * 7):
+        gather("VS"[i % 2], ("YB", lo, lo + w), ("R", 0, 2052), ("INV", lo // 16, (lo + w) // 16))
+        stores.append(op(rec, "Y", lambda e, lo=lo, w=w: e.dma_start(T.y[:, lo:lo + w], t("YB", lo, lo + w)),
+                         [("YB", lo, lo + w)], (), "d"))
+        lo += w
+    op(rec, "Y", None, (), (), "n", stores)
+    emit(rec, g, T)

@@ -2,23 +2,25 @@ from concourse.bass import DstId, RemoteDMATransfer
 from concourse.mybir import AluOpType as Op, ActivationFunctionType as AF
 
 WORLD = 256
+DIRECT = (3,)
+VIAMATE = (0, 2, 3)
 SCRATCH, AT = {}, {}
 for _d, _s in (("float32", "WB:1024 WS:1024 XB:4352 YB:4096 R:2064 VB:512 VS:1792 RES:512 GTE:8 LST:128 GMT:16"),
-               ("int32", "PKI:8"), ("uint16", "OFF:128 PREV:128 INV:256 XOFF:128"), ("bfloat16", "MAP:4352 GT:2048")):
+               ("int32", "PKI:8"), ("uint16", "OFF:128 PREV:128 INV:256 XOFF:128"), ("bfloat16", "MAP:4352 GT:1024")):
     for _x in _s.split():
         _n, _w = _x.split(":")
         SCRATCH[_n] = ("sbuf", [128, int(_w)], _d)
         AT[_n] = (_n, 0, int(_w))
 for _b, _d, _s in (
-        ("TF", "float32", "GB:512 HS:1024 PF:1 P16F:1 PMF:1 PMF16:1 PGF:1 P8F:1 IOM:128 IO16:16 IOC:16 L0:16 TOKM:8 SO:64 SA:32 "
-         "SB:16 D16:8 COLF:8 VAL:8 LT:1024 RH:128 RG:128 RM16:128 SELT:128 MSI:256 MSK:256 SGA:128 SGB:128 REPG:256 "
-         "GX:256 XF:128 DMI:128 DM:128 XM:128 XA:64 XC:32 XD:16 PCI:8 K128:256 BASE:128 ZA:128 ZB:128 ZC:128 ZD:128 "
-         "ZE:128 ZT1:64 ZT2:32 ZT3:16 PT:16 YA:256 YBB:256 YC:256 YT1:128 YT2:64 YT3:32 IT:32 C8F:16 M8I:256 M8:256 "
-         "P16I:128 P16:128 PTR:128 PTM:128 ITR:256 ITM:256"),
-        ("TI", "int32", "PM4:4 PM4b:4 PMI:1 PGI:1 P8I:1 OCOL:64 N8:64 OW16:8 OW256:8 TOKI:8 OWR:64 SEL:8 H16:8 C16I:16 "
-         "PGW:128 PGW4:128 C8I:16"),
-        ("TU", "uint16", "RO8:4 C16:16 E16:16 C8:16"),
-        ("TB", "bfloat16", "SM:64 TRI:128 ONES:128 OB:66 EX:64 VALS:256 PICK:8")):
+        ("TF", "float32", "GB:512 HS:1024 PF:1 P16F:1 PMF:1 PMF16:1 PGF:1 P8F:1 I8F:1 IOM:128 IOC:16 L0:16 SO:64 SA:32 "
+         "SB:16 COLF:8 HI:8 LO:8 IOCQ:128 LTF:1024 RG:128 RM16:128 SELT:128 MSI:256 MSK:256 SGA:128 SGB:128 "
+         "GX:256 XF:128 PCI:8 K128:256 BASE:64 ZA:64 ZB:64 ZC:64 ZD:64 "
+         "ZE:64 ZT1:32 ZT2:16 ZT3:8 YA:256 YBB:256 YC:256 YT1:128 YT2:64 YT3:32 C8F:16 M8I:256 M8:256 "
+         "P16I:128 P16:128 PTM:64 ITM:256"),
+        ("TI", "int32", "PM4:4 PM4b:4 PMI:1 PGI:1 P8I:1 B8I:1 OCOL:64 N8:64 OW16:8 OW256:8 TOKH:8 TOKL:8 OWR:64 SEL:8 H16:8 "
+         "C16I:16 PGW:128 PGW4:128 C8I:16 XPI:4"),
+        ("TU", "uint16", "RO8:4 C16:16 E16:16 C8:16 PCOL:4 XPO:4 XP:64"),
+        ("TB", "bfloat16", "SM:64 TRI:128 ONES:128 OB:66 EX:64 VALS:256 PICK:8 IOMB:128 EQ:128 RHH:128 RHL:128 LT:1024 D16:8")):
     _o = 0
     for _x in _s.split():
         _n, _w = _x.split(":")
@@ -29,7 +31,7 @@ for _i in range(8):
     SCRATCH["p%d" % _i] = ("psum", [128, 512], "float32")
     AT["p%d" % _i] = ("p%d" % _i, 0, 512)
 SEMAPHORES = (["aW%d" % f for f in range(4)] + ["aS%d" % f for f in range(4)] + ["aR%d" % n for n in range(16)]
-              + ["aL", "aG", "aV0", "aV1", "aX", "aP", "aI", "ls"] + ["q%d" % i for i in range(32)])
+              + ["aL", "aG", "aV0", "aV1", "aX", "aP0", "aP1", "aI", "ls"] + ["q%d" % i for i in range(32)])
 
 
 def bits(mask):
@@ -137,10 +139,9 @@ def make_plan(T, topo):
             place[(k, e)] = c
             third[(k, e)] = h
         spread[r] = port
-        x = [c for c in range(WORLD) if topo.same_plane(c, rc) and topo.host(c) == topo.host(rc)
-             and topo.die(c) == topo.die(rc) and key(c) not in chips and c not in used][0]
-        used.add(x)
-        index[r] = x
+        index[r] = [c for c in range(WORLD) if topo.same_plane(c, rc) and topo.host(c) == topo.host(rc)
+                    and topo.die(c) == topo.die(rc) and key(c) not in chips and c not in used][:2]
+        used.update(index[r])
     pos = {}
     for r, rc in enumerate(cores):
         k = key(rc)
@@ -201,9 +202,13 @@ def rank_program(g, core, T, topo):
         else:
             V(lambda e: e.tensor_scalar(t(*out), t(*in0), sc[0], sc[1], op0, op1), rd, [out])
 
-    def tt(out, a, b, o):
+    def tt(out, a, b, o, off=None):
         out, a, b = full(out), full(a), full(b)
-        V(lambda e: e.tensor_tensor(t(*out), t(*a), t(*b), o), [a, b], [out])
+        if off is None:
+            V(lambda e: e.tensor_tensor(t(*out), t(*a), t(*b), o), [a, b], [out])
+        else:
+            off = full(off)
+            V(lambda e: e.tensor_tensor(t(*out), t(*a).indirect(t(*off)), t(*b), o), [a, b, off], [out])
 
     def cp(out, a):
         out, a = full(out), full(a)
@@ -234,41 +239,43 @@ def rank_program(g, core, T, topo):
         cp("PGF", "PGI")
 
     for r in range(N):
-        if index[r] != core:
+        if core not in index[r]:
             continue
+        half = index[r].index(core)
         ob = bits(topo.mask(core, cores[r]))
         arrive("aX", len(ob), [al("XOFF")])
         part_consts()
-        iota("DMI", [[1, 8], [0, 16]])
         iota("VALS", [[1, 256]])
         iota("PCI", [[16, 8]])
-        iota("K128", [[0, 32], [128, 8]], 1)
-        iota("BASE", [[128, 8], [1024, 2], [0, 8]])
+        iota("XPI", [[32, 4]], 8 * half)
         iota("C8I", [[2, 16]])
+        iota("K128", [[0, 32], [128, 8]], 1)
+        iota("BASE", [[128, 8], [0, 8]], 1024 * half)
         iota("M8I", [[0, 32], [1, 8]])
         iota("P16I", [[0, 8], [1, 16]])
         fill("MAP", -32768.0)
-        ts("DM", "DMI", "PGF", None, Op.is_equal)
+        cp("PCOL", "PM4")
         ts("PICK", "PCI", "PF", None, Op.is_equal)
+        ts("B8I", ("PM4", 0, 1), 8, None, Op.bitwise_and)
+        tt("I8F", "PMI", "B8I", Op.add)
+        ts("XPO", "XPI", "I8F", None, Op.add)
         ts("P8I", ("PM4", 0, 1), 3, 1, Op.logical_shift_right, Op.bitwise_and)
         cp("P8F", "P8I")
-        ts("C8F", "C8I", "P8F", None, Op.add)
-        cp("C8", "C8F")
+        ts("C8", "C8I", "P8F", None, Op.add)
         ts("M8", "M8I", "PGF", None, Op.is_equal)
         ts("P16", "P16I", "PMF", None, Op.is_equal)
         cp("XF", "XOFF")
-        tt("XM", "XF", "DM", Op.mult)
-        tt("XA", ("XM", 0, 64), ("XM", 64, 128), Op.add)
-        tt("XC", ("XA", 0, 32), ("XA", 32, 64), Op.add)
-        tt("XD", ("XC", 0, 16), ("XC", 16, 32), Op.add)
-        cp("E16", "XD")
+        gather("V", "E16", "XF", ("PCOL", 0, 1))
+        gather("V", "XP", "XF", "XPO")
         V(lambda e: e.tensor_copy(t("MAP").indirect(t("E16")), t("VALS")), [al("VALS"), al("E16"), al("MAP")], [al("MAP")])
-        for b in range(32):
-            mm(("p0", 8 * b, 8 * b + 8), ("MAP", 128 * b, 128 * b + 128), "PICK", True, True)
-        for h in range(4):
-            gather("SV"[h % 2], ("GT", 512 * h, 512 * h + 512), "MAP", ("XOFF", 32 * h, 32 * h + 32))
-        for b in range(16):
+        for h in range(2):
+            gather("SV"[h], ("GT", 512 * h, 512 * h + 512), "MAP", ("XP", 32 * h, 32 * h + 32))
+        for b in range(8):
             mm(("p1", 8 * b, 8 * b + 8), ("GT", 128 * b, 128 * b + 128), "PICK", True, True)
+
+        def tokens(blocks):
+            for b in blocks:
+                mm(("p0", 8 * b, 8 * b + 8), ("MAP", 128 * b, 128 * b + 128), "PICK", True, True)
 
         def tree(src, a, n):
             for d in a:
@@ -277,25 +284,27 @@ def rank_program(g, core, T, topo):
                   [al(src)], [al(d)])
                 src = d
 
-        def wrap(cols, src, rep, prod, bank, n, out, sem):
-            ts(cols, src, 0.0, 3.0, Op.max, Op.add)
-            gather("V", rep, cols, ("C8", 0, n // 16))
-            tt(prod, rep, ("M8", 0, n), Op.mult)
+        def wrap(src, prod, bank, n, out, sem):
+            tt(prod, src, ("M8", 0, n), Op.mult, ("C8", 0, n // 16))
             mm((bank, 0, n), "P16", prod, True, True)
-            cp(out, (bank, 0, n))
-            send([(ob, sem, t(out), [(cores[r], t(out))])], [al(out)])
-        ts("ZA", ("p1", 0, 128), 127.5, 896.0, Op.is_gt, Op.mult)
-        tt("ZB", ("p1", 0, 128), "ZA", Op.add)
-        tt("ZC", "ZB", ("K128", 0, 128), Op.add)
+            ts(out, (bank, 0, n), 0.0, 3.0, Op.max, Op.add)
+            send([(ob, sem, t(*out), [(cores[r], t(*out))])], [out])
+        if half == 0:
+            tokens(range(16))
+        ts("ZA", ("p1", 0, 64), 127.5, 896.0, Op.is_gt, Op.mult)
+        tt("ZB", ("p1", 0, 64), "ZA", Op.add)
+        tt("ZC", "ZB", ("K128", 0, 64), Op.add)
         tt("ZD", "ZC", "BASE", Op.is_le)
         tt("ZE", "ZD", "ZC", Op.mult)
-        tree("ZE", ("ZT1", "ZT2", "ZT3"), 128)
-        wrap("PT", "ZT3", "PTR", "PTM", "p2", 128, "PREV", "aP")
-        ts("YA", ("p0", 0, 256), 127.5, 896.0, Op.is_gt, Op.mult)
-        tt("YBB", ("p0", 0, 256), "YA", Op.add)
-        tt("YC", "YBB", "K128", Op.add)
-        tree("YC", ("YT1", "YT2", "YT3"), 256)
-        wrap("IT", "YT3", "ITR", "ITM", "p3", 256, "INV", "aI")
+        tree("ZE", ("ZT1", "ZT2", "ZT3"), 64)
+        wrap("ZT3", "PTM", "p2", 64, ("PREV", 64 * half, 64 * half + 64), "aP%d" % half)
+        if half == 0:
+            tokens(range(16, 32))
+            ts("YA", ("p0", 0, 256), 127.5, 896.0, Op.is_gt, Op.mult)
+            tt("YBB", ("p0", 0, 256), "YA", Op.add)
+            tt("YC", "YBB", "K128", Op.add)
+            tree("YC", ("YT1", "YT2", "YT3"), 256)
+            wrap("YT3", "ITM", "p3", 256, al("INV"), "aI")
         emit(rec, g, T)
         return
     if key not in chips:
@@ -314,7 +323,7 @@ def rank_program(g, core, T, topo):
     if me is None:
         near = topo.mates(core, home) or topo.same_plane(core, home)
         for f in range(4):
-            arrive("aW%d" % f, half if near else len(OFFB), [("WB", 256 * f, 256 * f + 256)])
+            arrive("aW%d" % f, half if near and f not in DIRECT else len(OFFB), [("WB", 256 * f, 256 * f + 256)])
             if spread_for:
                 arrive("aS%d" % f, len(HIB), [("WS", 256 * f, 256 * f + 256)])
         arrive("aG", len(OFFB), [al("GMT")])
@@ -324,7 +333,8 @@ def rank_program(g, core, T, topo):
     if me is not None:
         pos = allpos[me]
         arrive("aL", len(OFFB) * (N - 2) + len(HIB), [("LST", 16 * pos[e], 16 * pos[e] + 16) for e in range(N) if e != me])
-        arrive("aP", len(OFFB), [al("PREV")])
+        for p in range(2):
+            arrive("aP%d" % p, len(OFFB), [("PREV", 64 * p, 64 * p + 64)])
         arrive("aI", len(OFFB), [al("INV")])
         for n in range(16):
             for e in range(N):
@@ -332,23 +342,31 @@ def rank_program(g, core, T, topo):
                     arrive("aR%d" % n, len(ONB) if n >= 8 or e in two else len(ONB) // 2, [("R", 4 + 128 * n, 132 + 128 * n)])
 
     def gate_iotas():
-        iota("C16I", [[1, 16]])
         iota("MSI", [[0, 16], [1, 16]])
         iota("PGW", [[0, 128]], 0, 1)
 
     def gate_consts():
-        cp("C16", "C16I")
         ts("MSK", "MSI", "PMF", None, Op.is_equal)
         ts("PGW4", "PGW", 4, None, Op.logical_shift_right)
         ts("SGA", "PGW4", float(two[0]), None, Op.is_equal)
         ts("SGB", "PGW4", float(two[1]), None, Op.is_equal)
 
     def gates_prepare():
-        gather("V", "REPG", "GMT", "C16")
-        tt("GX", "REPG", "MSK", Op.mult)
+        tt("GX", "GMT", "MSK", Op.mult, "C16")
+
+    def gates_spread():
+        for p in range(2):
+            for a in range(2):
+                mm(("p7", 256 * p + 128 * a, 256 * p + 128 * a + 128), "SG" + "AB"[a],
+                   ("GX", 128 * p, 128 * p + 128), True, True)
+        cp("GB", "p7")
 
     order = [third[(key, E)], 1 - third[(key, E)]]
     blocks = [(0, 256)] + [(256 + 128 * a, 384 + 128 * a) for a in order]
+
+    def tile(layer, f):
+        c = 512 * (f // 2) + 256 * layer + 128 * (f % 2)
+        return ("WB", c, c + 128)
 
     def expert():
         units = [(b, f) for b in range(3) for f in range(4)]
@@ -358,23 +376,17 @@ def rank_program(g, core, T, topo):
             b, f = units[u]
             n = blocks[b][1] - blocks[b][0]
             s = 256 * (u % 4)
-            mm(("p%d" % (4 + b), 0, n), ("WB", 256 * f + 128, 256 * f + 256), ("HS", s, s + n), f == 0, f == 3)
+            mm(("p%d" % (4 + b), 0, n), tile(1, f), ("HS", s, s + n), f == 0, f == 3)
         for u, (b, f) in enumerate(units):
             lo, hi = blocks[b]
             n = hi - lo
             h = "p%d" % (u % 4)
             s = 256 * (u % 4)
-            mm((h, 0, n), ("WB", 256 * f, 256 * f + 128), ("VB", lo, hi), True, True)
+            mm((h, 0, n), tile(0, f), ("VB", lo, hi), True, True)
             op(rec, "S", lambda e, h=h, n=n, s=s: e.activation(t("HS", s, s + n), t(h, 0, n), AF.Relu),
                [(h, 0, n)], [("HS", s, s + n)])
             if u >= LAG:
                 l2(u - LAG)
-            if u == 4:
-                for p in range(2):
-                    for a in range(2):
-                        mm(("p7", 256 * p + 128 * a, 256 * p + 128 * a + 128), "SG" + "AB"[a],
-                           ("GX", 128 * p, 128 * p + 128), True, True)
-                cp("GB", "p7")
         for u in range(len(units) - LAG, len(units)):
             l2(u)
 
@@ -387,32 +399,36 @@ def rank_program(g, core, T, topo):
 
     if me is None:
         part_consts()
+        iota("C16I", [[1, 16]])
         gate_iotas()
+        cp("C16", "C16I")
         gate_consts()
         gates_prepare()
+        gates_spread()
 
         def forward(f):
             w, d = t("WS", 256 * f, 256 * f + 256), t("WB", 256 * f, 256 * f + 256)
             to = [place[(k, spread_for[0])] for k in chips if k != key]
             m = [c for c in to if topo.mates(core, c)][0]
             s = [c for c in to if topo.same_plane(core, c)][0]
-            send([(OFFB[:half], "aW%d" % f, w, [(m, d)]), (OFFB[half:], "aW%d" % f, w, [(s, d)])],
-                 [("WS", 256 * f, 256 * f + 256)])
+            if f in DIRECT:
+                trs = [(OFFB, "aW%d" % f, w, [(s, d)])]
+            else:
+                trs = [(OFFB[:half], "aW%d" % f, w, [(m, d)]), (OFFB[half:], "aW%d" % f, w, [(s, d)])]
+            send(trs, [("WS", 256 * f, 256 * f + 256)])
 
         def relay(f):
             w = t("WB", 256 * f, 256 * f + 256)
             c = [x for x in elsewhere if not topo.mates(home, x) and not topo.same_plane(home, x)][0]
             send([(OFFB, "aW%d" % f, w, [(c, w)])], [("WB", 256 * f, 256 * f + 256)])
         if spread_for:
-            forward(0)
-            forward(1)
-            forward(2)
-            relay(1)
-            forward(3)
-            relay(3)
+            for f in range(4):
+                forward(f)
+                if f >= 2 and f - 1 not in VIAMATE:
+                    relay(f - 1)
         elif topo.mates(core, home):
-            relay(0)
-            relay(2)
+            for f in VIAMATE:
+                relay(f)
         expert()
         for b, (lo, hi) in enumerate(blocks):
             tt(("RES", lo, hi), ("p%d" % (4 + b), 0, hi - lo), ("GB", lo, hi), Op.mult)
@@ -429,33 +445,33 @@ def rank_program(g, core, T, topo):
     mya = two.index(me)
     oth = 1 - mya
 
-    def load(out, src):
-        return op(rec, "Y", lambda e: e.dma_start(t(*out), src), (), [out], "d")
+    def load(out, src, deps=()):
+        return op(rec, "Y", lambda e: e.dma_start(t(*out), src), (), [out], "d", deps)
     load(al("PKI"), T.pick[:])
     load(al("GTE"), T.gate[:])
-    for f in range(4):
-        load(("WB", 256 * f, 256 * f + 128), T.w1[:, 128 * f:128 * f + 128])
-        load(("WB", 256 * f + 128, 256 * f + 256), T.w2[:, 128 * f:128 * f + 128])
-        load(("XB", 1024 * f, 1024 * f + 1024), T.x[:, 1024 * f:1024 * f + 1024])
+    for h in range(2):
+        load(("WB", 512 * h, 512 * h + 256), T.w1[:, 256 * h:256 * h + 256])
+        last = load(("WB", 512 * h + 256, 512 * h + 512), T.w2[:, 256 * h:256 * h + 256])
+    load(("XB", 0, 2048), T.x[:, 0:2048])
+    load(("XB", 2048, 4096), T.x[:, 2048:4096], [last])
 
     iota("PM4", [[0, 4]], 0, 1)
     iota("OCOL", [[16, 8], [0, 8]])
     iota("N8", [[0, 8], [1, 8]])
     iota("IOM", [[16, 128]])
-    iota("IO16", [[1, 16]])
+    iota("C16I", [[1, 16]])
+    iota("IOCQ", [[0, 8], [1, 16]])
     iota("IOC", [[1, 16]], 4096)
-    iota("RM16", [[0, 8], [1, 16]], 16 * me)
-    gate_iotas()
     fill(("OB", 0, 2), 0.0)
     fill("ONES", 1.0)
     ts("PM4b", "PM4", 7, None, Op.bitwise_and)
     cp("RO8", "PM4b")
-    cp("PF", ("PM4", 0, 1))
     ts("P16F", ("PM4", 0, 1), 16.0, None, Op.mult)
-    ts("PMI", ("PM4", 0, 1), 15, None, Op.bitwise_and)
     ts("SM", "N8", 0.0, None, Op.is_gt)
     ts("TRI", "IOM", "P16F", None, Op.is_gt)
-    cp("PMF", "PMI")
+    cp("IOMB", "IOM")
+    ts("PMI", ("PM4", 0, 1), 15, None, Op.bitwise_and)
+    cp("C16", "C16I")
     ts("PMF16", "PMI", 16.0, None, Op.mult)
     ts("L0", "IOC", "PMF16", None, Op.add)
 
@@ -466,46 +482,57 @@ def rank_program(g, core, T, topo):
     V(lambda e: e.tensor_tensor_scan(t("EX"), t("OB", 1, 65), t("SM"), 0.0, Op.add, Op.mult), [al("OB"), al("SM")], [al("EX")])
     mm(("p0", 0, 64), "ONES", "EX", False, True)
     ts("OW256", "PKI", 4, 0xF00, Op.logical_shift_right, Op.bitwise_and)
-    ts("TOKI", "PKI", 4095, None, Op.bitwise_and)
-    ts("TOKM", "TOKI", 4096.0, None, Op.subtract)
+    ts("TOKH", "PKI", 0xFC0, None, Op.bitwise_and)
+    ts("TOKL", "PKI", 0x3F, None, Op.bitwise_and)
+    ts("HI", "TOKH", 4096.0, None, Op.subtract)
     tt("SO", ("p0", 0, 64), ("OB", 2, 66), Op.mult)
     tt("SA", ("SO", 0, 32), ("SO", 32, 64), Op.add)
     tt("SB", ("SA", 0, 16), ("SA", 16, 32), Op.add)
     tt("SEL", ("SB", 0, 8), ("SB", 8, 16), Op.add)
     ts("H16", "SEL", 0xF0, None, Op.bitwise_and)
-    tt("VAL", "TOKM", "SEL", Op.subtract)
+    tt("LO", "TOKL", "SEL", Op.subtract)
     tt("D16", "H16", "OW256", Op.add)
     tt("COLF", "SEL", "H16", Op.subtract)
+    tt("EQ", "COLF", "IOCQ", Op.is_equal, ("C16", 0, 8))
+    tt("RHH", "HI", "EQ", Op.mult, ("C16", 0, 8))
+    tt("RHL", "LO", "EQ", Op.mult, ("C16", 0, 8))
     for q in range(8):
-        ts(("RH", 16 * q, 16 * q + 16), "IO16", ("COLF", q, q + 1), ("VAL", q, q + 1), Op.is_equal, Op.mult)
-        ts(("LT", 128 * q, 128 * q + 128), "IOM", ("D16", q, q + 1), None, Op.is_equal)
-        mm(("p1", 0, 16), ("LT", 128 * q, 128 * q + 128), ("RH", 16 * q, 16 * q + 16), q == 0, q == 7)
+        lt = ("LT", 128 * q, 128 * q + 128)
+        ts(lt, "IOMB", ("D16", q, q + 1), None, Op.is_equal)
+        mm(("p1", 0, 16), lt, ("RHH", 16 * q, 16 * q + 16), q == 0, False)
+        mm(("p1", 0, 16), lt, ("RHL", 16 * q, 16 * q + 16), False, q == 7)
     mine = ("LST", 16 * pos[me], 16 * pos[me] + 16)
     tt(mine, ("p1", 0, 16), "L0", Op.add)
 
-    def weights(f):
+    for f in range(4):
         w = ("WB", 256 * f, 256 * f + 256)
-        send([(HIB, "aS%d" % f, t(*w), [(spread[me], t("WS", w[1], w[2]))])], [w])
-    weights(0)
-    weights(1)
+        trs = [(HIB, "aS%d" % f, t(*w), [(spread[me], t("WS", w[1], w[2]))])]
+        if f in DIRECT:
+            trs.append((OFFB, "aW%d" % f, t(*w), [(c, t(*w)) for c in elsewhere if topo.mates(core, c)]))
+        send(trs, [w])
     to = [(e, t("LST", 16 * allpos[e][me], 16 * allpos[e][me] + 16)) for e in list(range(me + 1, N)) + list(range(me))]
     send([(OFFB, "aL", t(*mine), [(cores[e], d) for e, d in to if e not in two]),
           (HIB, "aL", t(*mine), [(cores[e], d) for e, d in to if e in two])], [mine])
-    weights(2)
-    weights(3)
+    iota("RM16", [[0, 8], [1, 16]], 16 * me)
+    gate_iotas()
 
+    cp("PF", ("PM4", 0, 1))
     ts("SELT", "RM16", "PF", None, Op.is_equal)
+    tt("RG", "GTE", "EQ", Op.mult, ("C16", 0, 8))
+    op(rec, "S", lambda e: e.activation(t("LTF"), t("LT"), AF.Copy), [al("LT")], [al("LTF")])
     for q in range(8):
-        ts(("RG", 16 * q, 16 * q + 16), "IO16", ("COLF", q, q + 1), ("GTE", q, q + 1), Op.is_equal, Op.mult)
-        mm(("p2", 0, 16), ("LT", 128 * q, 128 * q + 128), ("RG", 16 * q, 16 * q + 16), q == 0, q == 7)
-    cp("GMT", ("p2", 0, 16))
+        mm(("p2", 0, 16), ("LTF", 128 * q, 128 * q + 128), ("RG", 16 * q, 16 * q + 16), q == 0, q == 7)
     fill(("XB", 4096, 4352), 0.0)
     fill(("R", 0, 4), 0.0)
+    cp("GMT", ("p2", 0, 16))
+    cp("PMF", "PMI")
     gate_consts()
     gates_prepare()
+    send([(OFFB, "aG", t("GMT"), [(c, t("GMT")) for c in elsewhere])], [al("GMT")])
 
     mm(("p3", 0, 128), "SELT", "LST", True, True)
     cp("OFF", ("p3", 0, 128))
+    send([(OFFB, "aX", t("OFF"), [(c, t("XOFF")) for c in index[me]])], [al("OFF")])
     others = [e for e in range(N) if e != me]
     crossing = [e for e in others if across(place[(key, e)])]
     staying = [e for e in others if e not in crossing]
@@ -521,10 +548,7 @@ def rank_program(g, core, T, topo):
             if e != me:
                 trs.append((engines[e], "aV%d" % p, t(*s), [(place[(key, e)], t("VB", v, v + 128))]))
         send(trs, [("VS", 896 * p, 896 * p + 896)])
-        if p == 0:
-            send([(OFFB, "aX", t("OFF"), [(index[me], t("XOFF"))])], [al("OFF")])
-            send([(OFFB, "aG", t("GMT"), [(c, t("GMT")) for c in elsewhere])], [al("GMT")])
-
+    gates_spread()
     expert()
 
     def scale(b, a):
@@ -542,11 +566,8 @@ def rank_program(g, core, T, topo):
     def chain(n):
         if n == 0:
             return
-        k, p = n % 8, n // 8
         u = 4 + 128 * n
-        V(lambda e: e.tensor_tensor(t("R", u, u + 128), t("R", 0, u).indirect(t("PREV", 16 * k + 8 * p, 16 * k + 8 * p + 8)),
-                                    t("R", u, u + 128), Op.add),
-          [("R", 0, u + 128), al("PREV")], [("R", u, u + 128)])
+        tt(("R", u, u + 128), ("R", 0, u), ("R", u, u + 128), Op.add, ("PREV", 8 * n, 8 * n + 8))
     scale(0, oth)
     scale(0, mya)
     scale(1, oth)
@@ -557,8 +578,10 @@ def rank_program(g, core, T, topo):
         chain(n)
     lo = 0
     stores = []
-    for i, w in enumerate([256, 256] + [512] * 7):
-        gather("VS"[i % 2], ("YB", lo, lo + w), ("R", 0, 2052), ("INV", lo // 16, (lo + w) // 16))
+    for w in (256, 512, 1024, 1280, 1024):
+        for i in range(2):
+            a = lo + i * w // 2
+            gather("VS"[i], ("YB", a, a + w // 2), ("R", 0, 2052), ("INV", a // 16, (a + w // 2) // 16))
         stores.append(op(rec, "Y", lambda e, lo=lo, w=w: e.dma_start(T.y[:, lo:lo + w], t("YB", lo, lo + w)),
                          [("YB", lo, lo + w)], (), "d"))
         lo += w

from concourse.bass import DstId, RemoteDMATransfer
from concourse.mybir import AluOpType as Op, ActivationFunctionType as AF

WORLD = 256
DIRECT = (3,)
VIAMATE = (0, 2, 3)
SCRATCH, AT = {}, {}
for _d, _s in (("float32", "WB:1024 WS:1024 XB:4352 YB:4096 R:2064 VB:512 VS:1792 RES:512 GTE:8 LST:128 GMT:16"),
               ("int32", "PKI:8"), ("uint16", "OFF:128 PREV:128 INV:256 XOFF:128"), ("bfloat16", "MAP:4352 GT:1024")):
    for _x in _s.split():
        _n, _w = _x.split(":")
        SCRATCH[_n] = ("sbuf", [128, int(_w)], _d)
        AT[_n] = (_n, 0, int(_w))
for _b, _d, _s in (
        ("TF", "float32", "GB:512 HS:1024 PF:1 P16F:1 PMF:1 PMF16:1 PGF:1 P8F:1 I8F:1 IOM:128 IOC:16 L0:16 SO:64 SA:32 "
         "SB:16 COLF:8 HI:8 LO:8 IOCQ:128 LTF:1024 RG:128 RM16:128 SELT:128 MSI:256 MSK:256 SGA:128 SGB:128 "
         "GX:256 XF:128 PCI:8 K128:256 BASE:64 ZA:64 ZB:64 ZC:64 ZD:64 "
         "ZE:64 ZT1:32 ZT2:16 ZT3:8 YA:256 YBB:256 YC:256 YT1:128 YT2:64 YT3:32 C8F:16 M8I:256 M8:256 "
         "P16I:128 P16:128 PTM:64 ITM:256"),
        ("TI", "int32", "PM4:4 PM4b:4 PMI:1 PGI:1 P8I:1 B8I:1 OCOL:64 N8:64 OW16:8 OW256:8 TOKH:8 TOKL:8 OWR:64 SEL:8 H16:8 "
         "C16I:16 PGW:128 PGW4:128 C8I:16 XPI:4"),
        ("TU", "uint16", "RO8:4 C16:16 E16:16 C8:16 PCOL:4 XPO:4 XP:64"),
        ("TB", "bfloat16", "SM:64 TRI:128 ONES:128 OB:66 EX:64 VALS:256 PICK:8 IOMB:128 EQ:128 RHH:128 RHL:128 LT:1024 D16:8")):
    _o = 0
    for _x in _s.split():
        _n, _w = _x.split(":")
        AT[_n] = (_b, _o, int(_w))
        _o += (int(_w) + 7) // 8 * 8
    SCRATCH[_b] = ("sbuf", [128, _o], _d)
for _i in range(8):
    SCRATCH["p%d" % _i] = ("psum", [128, 512], "float32")
    AT["p%d" % _i] = ("p%d" % _i, 0, 512)
SEMAPHORES = (["aW%d" % f for f in range(4)] + ["aS%d" % f for f in range(4)] + ["aR%d" % n for n in range(16)]
              + ["aL", "aG", "aV0", "aV1", "aX", "aP0", "aP1", "aI", "ls"] + ["q%d" % i for i in range(32)])


def bits(mask):
    return [1 << b for b in range(32) if mask >> b & 1]


def dep_scan(rec, q, rd, wr):
    deps = []
    ops = rec["ops"]
    inorder = q in ("V", "P", "S", "G")
    for regs, w in ((rd, False), (wr, True)):
        for name, lo, hi in regs:
            ps = name[0] == "p"
            for alo, ahi, aid, aw in rec["acc"].get(name, []):
                same = inorder and ops[aid]["q"] == q and ops[aid]["kind"] == "c"
                over = alo < hi and lo < ahi
                if same:
                    need = over and aw and not w
                elif ps:
                    need = True
                else:
                    need = over and (aw or w)
                if need and aid not in deps:
                    deps.append(aid)
    return deps


def op(rec, q, fn, rd=(), wr=(), kind="c", deps=(), sem=None, cnt=0):
    d = dep_scan(rec, q, rd, wr) if kind != "r" else []
    d += [x for x in deps if x not in d]
    me = len(rec["ops"])
    rec["ops"].append({"q": q, "fn": fn, "deps": d, "kind": kind, "sem": sem, "cnt": cnt})
    for regs, w in ((rd, False), (wr, True)):
        for name, lo, hi in regs:
            rec["acc"].setdefault(name, []).append((lo, hi, me, w))
    return me


def emit(rec, g, T):
    eng = {"V": g.vector, "P": g.tensor, "S": g.scalar, "Y": g.sync, "G": g}
    known = {q: set() for q in eng}
    after, plan, waited = {}, [], set()
    for i, o in enumerate(rec["ops"]):
        if o["kind"] == "r":
            after[i] = {i}
            continue
        k = known[o["q"]]
        ws = []
        for d in sorted(o["deps"], reverse=True):
            if d not in k:
                ws.append(d)
                k |= after[d]
                waited.add(d)
        after[i] = k | {i}
        plan.append((i, o, ws))
    taken = {o["sem"] for o in rec["ops"]} | {"ls"}
    pool = [s for s in reversed(SEMAPHORES) if s not in taken]
    sem, tails = {}, []
    for i, o in enumerate(rec["ops"]):
        assert o["kind"] != "r" or i in waited, "an arrival that nobody waits for"
        if i not in waited:
            continue
        if o["kind"] == "r":
            sem[i] = (T.sem[o["sem"]], o["cnt"])
            continue
        assert o["kind"] in ("c", "d"), "a send is never waited for"
        for x in tails:
            if x[0] in after[i] and x[3] == o["kind"]:
                break
        else:
            x = [None, 0, T.sem[pool[len(tails)]], o["kind"]]
            tails.append(x)
        x[0], x[1] = i, x[1] + (16 if o["kind"] == "d" else 1)
        sem[i] = (x[2], x[1])
    for i, o, ws in plan:
        e = eng[o["q"]]
        for d in ws:
            e.wait_ge(sem[d][0], sem[d][1])
        if o["fn"] is not None:
            ins = o["fn"](e)
            if i in sem:
                ins.then_inc(sem[i][0], 16 if o["kind"] == "d" else 1)
    if rec["ls"]:
        g.wait_ge(T.sem["ls"], rec["ls"])


def make_plan(T, topo):
    cores = T.cores
    R = range(len(cores))
    key = lambda c: (topo.host(c), topo.chip(c))
    chips = list(dict.fromkeys(key(c) for c in cores))
    place, spread, index, pair, third, used = {}, {}, {}, {}, {}, set()
    for r, rc in enumerate(cores):
        k = key(rc)
        pair[k] = [s for s in R if key(cores[s]) == k]
        peers = [c for c in range(WORLD) if key(c) == k and topo.die(c) == topo.die(rc) and c != rc]
        like = [e for e in R if e != r and topo.die(cores[e]) == topo.die(rc)]
        mate = [e for e in like if topo.mates(cores[e], rc)][0]
        plane = [e for e in like if topo.same_plane(cores[e], rc)][0]
        diag = [e for e in like if e not in (mate, plane)][0]
        port = [c for c in peers if topo.may_write(c, cores[mate])][0]
        rest = [c for c in peers if c != port]
        a = pair[k].index(r)
        for e, c, h in ((r, rc, 1 - a), (plane, port, a), (mate, rest[0], 1 - a), (diag, rest[1], a)):
            place[(k, e)] = c
            third[(k, e)] = h
        spread[r] = port
        index[r] = [c for c in range(WORLD) if topo.same_plane(c, rc) and topo.host(c) == topo.host(rc)
                    and topo.die(c) == topo.die(rc) and key(c) not in chips and c not in used][:2]
        used.update(index[r])
    pos = {}
    for r, rc in enumerate(cores):
        k = key(rc)
        a = pair[k].index(r)
        order = [e for e in R if third[(k, e)] == a] + [e for e in R if third[(k, e)] != a and e != r] + [r]
        pos[r] = {e: i for i, e in enumerate(order)}
    return key, chips, place, spread, index, pair, third, pos


def rank_program(g, core, T, topo):
    keyof, chips, place, spread, index, pair, third, allpos = make_plan(T, topo)
    key = keyof(core)
    me = T.rank_of(core)
    rec = {"ops": [], "acc": {}, "ls": 0}
    cores = T.cores
    N = len(cores)

    def t(name, lo=None, hi=None, step=1):
        b, o, n = AT[name]
        lo, hi = (0, n) if lo is None else (lo, hi)
        return T[b][:, o + lo:o + hi] if step == 1 else T[b][:, o + lo:o + hi:step]

    def al(name):
        return (name, 0, AT[name][2])

    def V(fn, rd, wr):
        return op(rec, "V", fn, rd, wr)

    def dst(c):
        rid, pid = topo.addr(c, core)
        return DstId(rid=rid, pnc=pid)

    def send(trs, rd):
        rec["ls"] += sum(len(x[0]) for x in trs)

        def fn(e):
            ts = [RemoteDMATransfer(dst_ids=[dst(c) for c, _ in ds], dma_engine_mask=sum(bs), remote_sem=T.sem[s],
                                    srcs=[src], dsts=[d for _, d in ds], alu_op=0) for bs, s, src, ds in trs]
            return e.remote_dma_fused(ts, local_sem=T.sem["ls"])
        op(rec, "G", fn, rd, (), "s")

    def arrive(sem, cnt, regs):
        op(rec, "R", None, (), regs, "r", (), sem, cnt)

    def iota(name, pattern, base=0, cm=0):
        op(rec, "G", lambda e: e.iota(t(name), pattern, base, cm, allow_small_or_imprecise_dtypes=True), (), [al(name)])

    def full(x):
        return al(x) if isinstance(x, str) else x

    def ts(out, in0, s1, s2, op0, op1=None):
        out, in0 = full(out), full(in0)
        sc = [full(s) for s in (s1, s2)]
        rd = [in0] + [s for s in sc if isinstance(s, tuple)]
        sc = [t(*s) if isinstance(s, tuple) else s for s in sc]
        if op1 is None:
            V(lambda e: e.tensor_scalar(t(*out), t(*in0), sc[0], None, op0), rd, [out])
        else:
            V(lambda e: e.tensor_scalar(t(*out), t(*in0), sc[0], sc[1], op0, op1), rd, [out])

    def tt(out, a, b, o, off=None):
        out, a, b = full(out), full(a), full(b)
        if off is None:
            V(lambda e: e.tensor_tensor(t(*out), t(*a), t(*b), o), [a, b], [out])
        else:
            off = full(off)
            V(lambda e: e.tensor_tensor(t(*out), t(*a).indirect(t(*off)), t(*b), o), [a, b, off], [out])

    def cp(out, a):
        out, a = full(out), full(a)
        V(lambda e: e.tensor_copy(t(*out), t(*a)), [a], [out])

    def fill(r, v):
        r = full(r)
        V(lambda e: e.memset(t(*r), v), [], [r])

    def mm(out, lhs, rhs, start, stop):
        lhs, rhs = full(lhs), full(rhs)
        op(rec, "P", lambda e: e.matmul(t(*out), t(*lhs), t(*rhs), start, stop), [lhs, rhs], [out])

    def gather(q, out, win, off):
        out, win, off = full(out), full(win), full(off)
        if q == "V":
            fn = lambda e: e.tensor_copy(t(*out), t(*win).indirect(t(*off)))
        else:
            fn = lambda e: e.activation(t(*out), t(*win).indirect(t(*off)), AF.Copy)
        op(rec, q, fn, [win, off], [out])

    def part_consts():
        iota("PM4", [[0, 4]], 0, 1)
        cp("PF", ("PM4", 0, 1))
        ts("PMI", ("PM4", 0, 1), 15, None, Op.bitwise_and)
        cp("PMF", "PMI")
        ts("PGI", ("PM4", 0, 1), 4, None, Op.logical_shift_right)
        cp("PGF", "PGI")

    for r in range(N):
        if core not in index[r]:
            continue
        half = index[r].index(core)
        ob = bits(topo.mask(core, cores[r]))
        arrive("aX", len(ob), [al("XOFF")])
        part_consts()
        iota("VALS", [[1, 256]])
        iota("PCI", [[16, 8]])
        iota("XPI", [[32, 4]], 8 * half)
        iota("C8I", [[2, 16]])
        iota("K128", [[0, 32], [128, 8]], 1)
        iota("BASE", [[128, 8], [0, 8]], 1024 * half)
        iota("M8I", [[0, 32], [1, 8]])
        iota("P16I", [[0, 8], [1, 16]])
        fill("MAP", -32768.0)
        cp("PCOL", "PM4")
        ts("PICK", "PCI", "PF", None, Op.is_equal)
        ts("B8I", ("PM4", 0, 1), 8, None, Op.bitwise_and)
        tt("I8F", "PMI", "B8I", Op.add)
        ts("XPO", "XPI", "I8F", None, Op.add)
        ts("P8I", ("PM4", 0, 1), 3, 1, Op.logical_shift_right, Op.bitwise_and)
        cp("P8F", "P8I")
        ts("C8", "C8I", "P8F", None, Op.add)
        ts("M8", "M8I", "PGF", None, Op.is_equal)
        ts("P16", "P16I", "PMF", None, Op.is_equal)
        cp("XF", "XOFF")
        gather("V", "E16", "XF", ("PCOL", 0, 1))
        gather("V", "XP", "XF", "XPO")
        V(lambda e: e.tensor_copy(t("MAP").indirect(t("E16")), t("VALS")), [al("VALS"), al("E16"), al("MAP")], [al("MAP")])
        for h in range(2):
            gather("SV"[h], ("GT", 512 * h, 512 * h + 512), "MAP", ("XP", 32 * h, 32 * h + 32))
        for b in range(8):
            mm(("p1", 8 * b, 8 * b + 8), ("GT", 128 * b, 128 * b + 128), "PICK", True, True)

        def tokens(blocks):
            for b in blocks:
                mm(("p0", 8 * b, 8 * b + 8), ("MAP", 128 * b, 128 * b + 128), "PICK", True, True)

        def tree(src, a, n):
            for d in a:
                n //= 2
                V(lambda e, s=src, d=d, n=n: e.tensor_tensor(t(d), t(s, 0, 2 * n, 2), t(s, 1, 2 * n, 2), Op.max),
                  [al(src)], [al(d)])
                src = d

        def wrap(src, prod, bank, n, out, sem):
            tt(prod, src, ("M8", 0, n), Op.mult, ("C8", 0, n // 16))
            mm((bank, 0, n), "P16", prod, True, True)
            ts(out, (bank, 0, n), 0.0, 3.0, Op.max, Op.add)
            send([(ob, sem, t(*out), [(cores[r], t(*out))])], [out])
        if half == 0:
            tokens(range(16))
        ts("ZA", ("p1", 0, 64), 127.5, 896.0, Op.is_gt, Op.mult)
        tt("ZB", ("p1", 0, 64), "ZA", Op.add)
        tt("ZC", "ZB", ("K128", 0, 64), Op.add)
        tt("ZD", "ZC", "BASE", Op.is_le)
        tt("ZE", "ZD", "ZC", Op.mult)
        tree("ZE", ("ZT1", "ZT2", "ZT3"), 64)
        wrap("ZT3", "PTM", "p2", 64, ("PREV", 64 * half, 64 * half + 64), "aP%d" % half)
        if half == 0:
            tokens(range(16, 32))
            ts("YA", ("p0", 0, 256), 127.5, 896.0, Op.is_gt, Op.mult)
            tt("YBB", ("p0", 0, 256), "YA", Op.add)
            tt("YC", "YBB", "K128", Op.add)
            tree("YC", ("YT1", "YT2", "YT3"), 256)
            wrap("YT3", "ITM", "p3", 256, al("INV"), "aI")
        emit(rec, g, T)
        return
    if key not in chips:
        return

    two = pair[key]
    E = [e for (k, e), c in place.items() if c == core][0]
    home = cores[E]
    elsewhere = [place[(k, E)] for k in chips if place[(k, E)] != home]
    OFFB = bits(topo.mask(core, [c for c in cores if keyof(c) != key and topo.may_write(core, c)][0]))
    ONB = bits(topo.mask(core, [place[(key, e)] for e in range(N) if e != E][0]))
    HIB = [b for b in ONB if b not in OFFB]
    half = len(OFFB) // 2
    spread_for = [r for r in two if spread[r] == core]

    if me is None:
        near = topo.mates(core, home) or topo.same_plane(core, home)
        for f in range(4):
            arrive("aW%d" % f, half if near and f not in DIRECT else len(OFFB), [("WB", 256 * f, 256 * f + 256)])
            if spread_for:
                arrive("aS%d" % f, len(HIB), [("WS", 256 * f, 256 * f + 256)])
        arrive("aG", len(OFFB), [al("GMT")])
    for p in range(2):
        froms = [a for a in range(2) if two[a] != me]
        arrive("aV%d" % p, 2 * len(froms), [("VB", 256 * p + 128 * a, 256 * p + 128 * a + 128) for a in froms])
    if me is not None:
        pos = allpos[me]
        arrive("aL", len(OFFB) * (N - 2) + len(HIB), [("LST", 16 * pos[e], 16 * pos[e] + 16) for e in range(N) if e != me])
        for p in range(2):
            arrive("aP%d" % p, len(OFFB), [("PREV", 64 * p, 64 * p + 64)])
        arrive("aI", len(OFFB), [al("INV")])
        for n in range(16):
            for e in range(N):
                if e != me and pos[e] == n % 8:
                    arrive("aR%d" % n, len(ONB) if n >= 8 or e in two else len(ONB) // 2, [("R", 4 + 128 * n, 132 + 128 * n)])

    def gate_iotas():
        iota("MSI", [[0, 16], [1, 16]])
        iota("PGW", [[0, 128]], 0, 1)

    def gate_consts():
        ts("MSK", "MSI", "PMF", None, Op.is_equal)
        ts("PGW4", "PGW", 4, None, Op.logical_shift_right)
        ts("SGA", "PGW4", float(two[0]), None, Op.is_equal)
        ts("SGB", "PGW4", float(two[1]), None, Op.is_equal)

    def gates_prepare():
        tt("GX", "GMT", "MSK", Op.mult, "C16")

    def gates_spread():
        for p in range(2):
            for a in range(2):
                mm(("p7", 256 * p + 128 * a, 256 * p + 128 * a + 128), "SG" + "AB"[a],
                   ("GX", 128 * p, 128 * p + 128), True, True)
        cp("GB", "p7")

    order = [third[(key, E)], 1 - third[(key, E)]]
    blocks = [(0, 256)] + [(256 + 128 * a, 384 + 128 * a) for a in order]

    def tile(layer, f):
        c = 512 * (f // 2) + 256 * layer + 128 * (f % 2)
        return ("WB", c, c + 128)

    def expert():
        units = [(b, f) for b in range(3) for f in range(4)]
        LAG = 2

        def l2(u):
            b, f = units[u]
            n = blocks[b][1] - blocks[b][0]
            s = 256 * (u % 4)
            mm(("p%d" % (4 + b), 0, n), tile(1, f), ("HS", s, s + n), f == 0, f == 3)
        for u, (b, f) in enumerate(units):
            lo, hi = blocks[b]
            n = hi - lo
            h = "p%d" % (u % 4)
            s = 256 * (u % 4)
            mm((h, 0, n), tile(0, f), ("VB", lo, hi), True, True)
            op(rec, "S", lambda e, h=h, n=n, s=s: e.activation(t("HS", s, s + n), t(h, 0, n), AF.Relu),
               [(h, 0, n)], [("HS", s, s + n)])
            if u >= LAG:
                l2(u - LAG)
        for u in range(len(units) - LAG, len(units)):
            l2(u)

    def rcol(a, p):
        n = 8 * p + allpos[two[a]][E]
        return n, 4 + 128 * n

    def across(c):
        return topo.die(c) != topo.die(core)

    if me is None:
        part_consts()
        iota("C16I", [[1, 16]])
        gate_iotas()
        cp("C16", "C16I")
        gate_consts()
        gates_prepare()
        gates_spread()

        def forward(f):
            w, d = t("WS", 256 * f, 256 * f + 256), t("WB", 256 * f, 256 * f + 256)
            to = [place[(k, spread_for[0])] for k in chips if k != key]
            m = [c for c in to if topo.mates(core, c)][0]
            s = [c for c in to if topo.same_plane(core, c)][0]
            if f in DIRECT:
                trs = [(OFFB, "aW%d" % f, w, [(s, d)])]
            else:
                trs = [(OFFB[:half], "aW%d" % f, w, [(m, d)]), (OFFB[half:], "aW%d" % f, w, [(s, d)])]
            send(trs, [("WS", 256 * f, 256 * f + 256)])

        def relay(f):
            w = t("WB", 256 * f, 256 * f + 256)
            c = [x for x in elsewhere if not topo.mates(home, x) and not topo.same_plane(home, x)][0]
            send([(OFFB, "aW%d" % f, w, [(c, w)])], [("WB", 256 * f, 256 * f + 256)])
        if spread_for:
            for f in range(4):
                forward(f)
                if f >= 2 and f - 1 not in VIAMATE:
                    relay(f - 1)
        elif topo.mates(core, home):
            for f in VIAMATE:
                relay(f)
        expert()
        for b, (lo, hi) in enumerate(blocks):
            tt(("RES", lo, hi), ("p%d" % (4 + b), 0, hi - lo), ("GB", lo, hi), Op.mult)
            trs = []
            for a in (0, 1) if b == 0 else (order[b - 1],):
                n, c0 = rcol(a, 0 if b == 0 else 1)
                eng = ONB if b else ONB[0::2] if across(cores[two[a]]) else ONB[1::2]
                s = 128 * a if b == 0 else lo
                trs.append((eng, "aR%d" % n, t("RES", s, s + 128), [(cores[two[a]], t("R", c0, c0 + 128))]))
            send(trs, [("RES", lo, hi)])
        emit(rec, g, T)
        return

    mya = two.index(me)
    oth = 1 - mya

    def load(out, src, deps=()):
        return op(rec, "Y", lambda e: e.dma_start(t(*out), src), (), [out], "d", deps)
    load(al("PKI"), T.pick[:])
    load(al("GTE"), T.gate[:])
    for h in range(2):
        load(("WB", 512 * h, 512 * h + 256), T.w1[:, 256 * h:256 * h + 256])
        last = load(("WB", 512 * h + 256, 512 * h + 512), T.w2[:, 256 * h:256 * h + 256])
    load(("XB", 0, 2048), T.x[:, 0:2048])
    load(("XB", 2048, 4096), T.x[:, 2048:4096], [last])

    iota("PM4", [[0, 4]], 0, 1)
    iota("OCOL", [[16, 8], [0, 8]])
    iota("N8", [[0, 8], [1, 8]])
    iota("IOM", [[16, 128]])
    iota("C16I", [[1, 16]])
    iota("IOCQ", [[0, 8], [1, 16]])
    iota("IOC", [[1, 16]], 4096)
    fill(("OB", 0, 2), 0.0)
    fill("ONES", 1.0)
    ts("PM4b", "PM4", 7, None, Op.bitwise_and)
    cp("RO8", "PM4b")
    ts("P16F", ("PM4", 0, 1), 16.0, None, Op.mult)
    ts("SM", "N8", 0.0, None, Op.is_gt)
    ts("TRI", "IOM", "P16F", None, Op.is_gt)
    cp("IOMB", "IOM")
    ts("PMI", ("PM4", 0, 1), 15, None, Op.bitwise_and)
    cp("C16", "C16I")
    ts("PMF16", "PMI", 16.0, None, Op.mult)
    ts("L0", "IOC", "PMF16", None, Op.add)

    ts("OW16", "PKI", 8, 0xF0, Op.logical_shift_right, Op.bitwise_and)
    gather("V", "OWR", "OW16", "RO8")
    tt(("OB", 2, 66), "OWR", "OCOL", Op.is_equal)
    mm(("p0", 0, 64), "TRI", ("OB", 2, 66), True, False)
    V(lambda e: e.tensor_tensor_scan(t("EX"), t("OB", 1, 65), t("SM"), 0.0, Op.add, Op.mult), [al("OB"), al("SM")], [al("EX")])
    mm(("p0", 0, 64), "ONES", "EX", False, True)
    ts("OW256", "PKI", 4, 0xF00, Op.logical_shift_right, Op.bitwise_and)
    ts("TOKH", "PKI", 0xFC0, None, Op.bitwise_and)
    ts("TOKL", "PKI", 0x3F, None, Op.bitwise_and)
    ts("HI", "TOKH", 4096.0, None, Op.subtract)
    tt("SO", ("p0", 0, 64), ("OB", 2, 66), Op.mult)
    tt("SA", ("SO", 0, 32), ("SO", 32, 64), Op.add)
    tt("SB", ("SA", 0, 16), ("SA", 16, 32), Op.add)
    tt("SEL", ("SB", 0, 8), ("SB", 8, 16), Op.add)
    ts("H16", "SEL", 0xF0, None, Op.bitwise_and)
    tt("LO", "TOKL", "SEL", Op.subtract)
    tt("D16", "H16", "OW256", Op.add)
    tt("COLF", "SEL", "H16", Op.subtract)
    tt("EQ", "COLF", "IOCQ", Op.is_equal, ("C16", 0, 8))
    tt("RHH", "HI", "EQ", Op.mult, ("C16", 0, 8))
    tt("RHL", "LO", "EQ", Op.mult, ("C16", 0, 8))
    for q in range(8):
        lt = ("LT", 128 * q, 128 * q + 128)
        ts(lt, "IOMB", ("D16", q, q + 1), None, Op.is_equal)
        mm(("p1", 0, 16), lt, ("RHH", 16 * q, 16 * q + 16), q == 0, False)
        mm(("p1", 0, 16), lt, ("RHL", 16 * q, 16 * q + 16), False, q == 7)
    mine = ("LST", 16 * pos[me], 16 * pos[me] + 16)
    tt(mine, ("p1", 0, 16), "L0", Op.add)

    for f in range(4):
        w = ("WB", 256 * f, 256 * f + 256)
        trs = [(HIB, "aS%d" % f, t(*w), [(spread[me], t("WS", w[1], w[2]))])]
        if f in DIRECT:
            trs.append((OFFB, "aW%d" % f, t(*w), [(c, t(*w)) for c in elsewhere if topo.mates(core, c)]))
        send(trs, [w])
    to = [(e, t("LST", 16 * allpos[e][me], 16 * allpos[e][me] + 16)) for e in list(range(me + 1, N)) + list(range(me))]
    send([(OFFB, "aL", t(*mine), [(cores[e], d) for e, d in to if e not in two]),
          (HIB, "aL", t(*mine), [(cores[e], d) for e, d in to if e in two])], [mine])
    iota("RM16", [[0, 8], [1, 16]], 16 * me)
    gate_iotas()

    cp("PF", ("PM4", 0, 1))
    ts("SELT", "RM16", "PF", None, Op.is_equal)
    tt("RG", "GTE", "EQ", Op.mult, ("C16", 0, 8))
    op(rec, "S", lambda e: e.activation(t("LTF"), t("LT"), AF.Copy), [al("LT")], [al("LTF")])
    for q in range(8):
        mm(("p2", 0, 16), ("LTF", 128 * q, 128 * q + 128), ("RG", 16 * q, 16 * q + 16), q == 0, q == 7)
    fill(("XB", 4096, 4352), 0.0)
    fill(("R", 0, 4), 0.0)
    cp("GMT", ("p2", 0, 16))
    cp("PMF", "PMI")
    gate_consts()
    gates_prepare()
    send([(OFFB, "aG", t("GMT"), [(c, t("GMT")) for c in elsewhere])], [al("GMT")])

    mm(("p3", 0, 128), "SELT", "LST", True, True)
    cp("OFF", ("p3", 0, 128))
    send([(OFFB, "aX", t("OFF"), [(c, t("XOFF")) for c in index[me]])], [al("OFF")])
    others = [e for e in range(N) if e != me]
    crossing = [e for e in others if across(place[(key, e)])]
    staying = [e for e in others if e not in crossing]
    engines = {e: ONB[0::2][2 * i:2 * i + 2] for i, e in enumerate(crossing)}
    engines.update({e: ONB[1::2][2 * i:2 * i + 2] for i, e in enumerate(staying)})
    for p in range(2):
        v = 256 * p + 128 * mya
        trs = []
        for i, e in enumerate(others + [me]):
            c = 16 * pos[e] + 8 * p
            s = ("VB", v, v + 128) if e == me else ("VS", 896 * p + 128 * i, 896 * p + 128 * i + 128)
            gather("VS"[i % 2], s, "XB", ("OFF", c, c + 8))
            if e != me:
                trs.append((engines[e], "aV%d" % p, t(*s), [(place[(key, e)], t("VB", v, v + 128))]))
        send(trs, [("VS", 896 * p, 896 * p + 896)])
    gates_spread()
    expert()

    def scale(b, a):
        p = 0 if b == 0 else 1
        o = ("p%d" % (4 + b), 128 * a, 128 * a + 128) if b == 0 else ("p%d" % (4 + b), 0, 128)
        gb = ("GB", 256 * p + 128 * a, 256 * p + 128 * a + 128)
        n, c0 = rcol(a, p)
        if a == mya:
            tt(("R", c0, c0 + 128), o, gb, Op.mult)
        else:
            s = ("RES", gb[1], gb[2])
            tt(s, o, gb, Op.mult)
            send([(ONB, "aR%d" % n, t(*s), [(cores[two[a]], t("R", c0, c0 + 128))])], [s])

    def chain(n):
        if n == 0:
            return
        u = 4 + 128 * n
        tt(("R", u, u + 128), ("R", 0, u), ("R", u, u + 128), Op.add, ("PREV", 8 * n, 8 * n + 8))
    scale(0, oth)
    scale(0, mya)
    scale(1, oth)
    for n in range(12):
        chain(n)
    scale(2, mya)
    for n in range(12, 16):
        chain(n)
    lo = 0
    stores = []
    for w in (256, 512, 1024, 1280, 1024):
        for i in range(2):
            a = lo + i * w // 2
            gather("VS"[i], ("YB", a, a + w // 2), ("R", 0, 2052), ("INV", a // 16, (a + w // 2) // 16))
        stores.append(op(rec, "Y", lambda e, lo=lo, w=w: e.dma_start(T.y[:, lo:lo + w], t("YB", lo, lo + w)),
                         [("YB", lo, lo + w)], (), "d"))
        lo += w
    op(rec, "Y", None, (), (), "n", stores)
    emit(rec, g, T)
